import numpy as np
import ml_dtypes


def mxq(x, axis, fmt="e4m3"):
    dtype, down = {"e4m3": (ml_dtypes.float8_e4m3fn, 7), "e5m2": (ml_dtypes.float8_e5m2, 14)}[fmt]
    v = np.moveaxis(np.asarray(x, np.float32).astype(ml_dtypes.bfloat16).astype(np.float64), axis, -1)
    blocks = v.reshape(v.shape[:-1] + (-1, 32))
    amax = np.abs(blocks).max(-1, keepdims=True)
    byte = np.maximum(np.where(amax > 0, np.frexp(amax)[1] - 1 + 127, 0) - down, 1)
    scale = np.exp2(byte - 127.0)
    codes = (blocks / scale).astype(np.float32).astype(dtype).astype(np.float64)
    return np.moveaxis((codes * scale).reshape(v.shape), -1, axis)


WIDE = False


def mx_kscale(k):
    if not WIDE:
        return np.ones(k)
    levels = np.array([10, -10, 5, -5, 0])
    if k % 512:
        return np.exp2(np.random.permutation(np.resize(levels, k // 32))).repeat(32)
    a = np.empty((k // 512, 16))
    for p in range(k // 512):
        a[p, :8] = np.random.permutation(np.resize(levels, 8))
        for g in range(8):
            far = levels[np.abs(levels - a[p, g]) >= 10]
            a[p, g + 8] = far[np.random.randint(len(far))]
    return np.exp2(a.ravel()).repeat(32)


def f64(x):
    return np.asarray(x).astype(np.float64)


def striped(idx):
    return np.tile(idx.reshape(-1, 16).T, (8, 1)).astype(np.uint16)


def unstriped(offs):
    return offs[:16].T.reshape(-1).astype(np.int64)


def striped8(idx):
    return np.concatenate([x.reshape(-1, 16).T for x in idx]).astype(np.uint16)


def runs(offs, k):
    lists = np.stack([offs[16 * r : 16 * r + 16].T.reshape(-1) for r in range(8)]).astype(np.int64)
    return lists[np.arange(k) % 512 // 64]


def pack_weight(w):
    k, n = w.shape
    w = f64(np.asarray(w, np.float32).astype(ml_dtypes.bfloat16)).reshape(k // 32, 32, n)
    amax = np.abs(w).max(1)
    byte = np.clip(np.where(amax > 0, np.frexp(amax)[1] - 1 + 127 - 7, 1), 1, 254)
    scaled = (w * np.exp2(127.0 - byte)[:, None, :]).reshape(k, n).astype(np.float32)
    words = np.ascontiguousarray(scaled.reshape(k // 512, 128, 4, n).transpose(0, 1, 3, 2)).astype(ml_dtypes.float8_e4m3fn).view(np.uint8)
    return words, np.ascontiguousarray(byte.astype(np.uint8).reshape(k // 512, 16, n))


def unpack_weight(words, scales):
    g, p, n, _ = words.shape
    vals = np.ascontiguousarray(words).view(ml_dtypes.float8_e4m3fn).astype(np.float64) * np.repeat(np.exp2(scales.astype(np.float64) - 127.0), 8, axis=1)[..., None]
    return vals.transpose(0, 1, 3, 2).reshape(g * 512, n)


def sigmoid(v):
    return 1.0 / (1.0 + np.exp(-np.maximum(v, -700.0)))

def planes(y):
    n, m = y.shape
    v = y.astype(np.float32).astype(ml_dtypes.bfloat16).astype(np.float64).reshape(n // 32, 32, m)
    top = np.abs(v).max(1)
    byte = np.clip(np.where(top > 0, np.frexp(top)[1] - 1 + 127 - 7, 1), 1, 254)
    codes = (v * np.exp2(127.0 - byte)[:, None, :]).reshape(n, m).astype(np.float32).astype(ml_dtypes.float8_e4m3fn).view(np.uint8)
    words = codes.reshape(n // 512, 128, 4, m).transpose(0, 1, 3, 2)
    return np.ascontiguousarray(words), np.ascontiguousarray(byte.astype(np.uint8).reshape(n // 512, 16, m))


K, T, S, V, H = 512, 2048, 512, 512, 512


def setup_inputs():
    n = np.random.standard_normal
    s = mx_kscale(K)[:, None]
    u = mx_kscale(S)
    packed_xT = pack_weight(n((K, T)) * s)
    packed_w1 = pack_weight(n((K, H)) / np.sqrt(K) / s)
    packed_w2 = pack_weight(n((K, H)) / np.sqrt(K) / s)
    return {
        "x_words": packed_xT[0],
        "x_scales": packed_xT[1],
        "w1_words": packed_w1[0],
        "w1_scales": packed_w1[1],
        "w2_words": packed_w2[0],
        "w2_scales": packed_w2[1],
        "ga": (np.random.uniform(0.5, 1.5, (H, 1)) * u[:, None]).astype(np.float32),
        "gb": (np.random.uniform(0.5, 1.5, (H, 1)) / u[:, None]).astype(np.float32),
        "offs": striped(np.random.permutation(T)[:S]),
        "two": striped(np.random.permutation(T)[:V]),
        "n1": striped8(np.stack([np.random.permutation(S) for _ in range(8)])),
        "n2": striped8(np.stack([np.random.permutation(S) for _ in range(8)])),
        "n3": striped8(np.stack([np.random.permutation(V) for _ in range(8)])),
        "n4": striped8(np.stack([np.random.permutation(V) for _ in range(8)])),
        "n5": striped8(np.stack([np.random.permutation(V) for _ in range(8)])),
        "n6": striped8(np.stack([np.random.permutation(V) for _ in range(8)])),
        "n7": striped8(np.stack([np.random.permutation(V) for _ in range(8)])),
    }


def reference(x_words, x_scales, w1_words, w1_scales, w2_words, w2_scales, ga, gb, offs, two, n1, n2, n3, n4, n5, n6, n7):
    xq = unpack_weight(x_words, x_scales)[:, unstriped(offs)]
    a = unpack_weight(w1_words, w1_scales).T @ xq
    st = a - (a[np.arange(H)[:, None], runs(n1, H)])
    z = f64(ga) * (st / (np.abs(st[np.arange(H)[:, None], runs(n2, H)]) + 0.5))
    x_two = unpack_weight(x_words, x_scales)[:, unstriped(two)]
    b = unpack_weight(w2_words, w2_scales).T @ x_two
    z2 = f64(gb) * (b[np.arange(H)[:, None], runs(n3, H)] - (b[np.arange(H)[:, None], runs(n4, H)]))
    s = 0.0625 * ((mxq(z, 0, "e4m3").T @ mxq(z2, 0, "e4m3")))
    pa = s[np.arange(S)[:, None], runs(n5, S)]
    out_0 = pa + (sigmoid(s[np.arange(S)[:, None], runs(n6, S)])) * (s[np.arange(S)[:, None], runs(n7, S)] - pa)
    return (out_0,) + planes(out_0)

@@ -1,0 +1,222 @@
+from contextlib import ExitStack
+
+import concourse.mybir as mybir
+
+K, T, S, V, H = 512, 2048, 512, 512, 512
+FLOPS = 2 * K * H * S + 2 * K * H * V + 2 * H * S * V
+
+F32 = mybir.dt.float32
+BF16 = mybir.dt.bfloat16
+I32 = mybir.dt.int32
+U32 = mybir.dt.uint32
+U16 = mybir.dt.uint16
+U8 = mybir.dt.uint8
+FP8X4 = mybir.dt.float8_e4m3fn_x4
+ALU = mybir.AluOpType
+ACT = mybir.ActivationFunctionType
+
+P = 128
+PACK = 4
+N = 512
+WINDOW = 2 * N
+HALF = N // 2
+TINY = 1e-37
+
+
+def load_scale_rows(queue, tile, first, scales):
+    for q in range(4):
+        queue.dma_start(
+            out=tile[32 * q + first : 32 * q + first + 4, :].bitcast(I32),
+            in_=scales[0, 4 * q : 4 * q + 4, :].bitcast(I32),
+        )
+
+
+def words_of(dram):
+    return dram[0].rearrange("p n t -> p (n t)").bitcast(I32)
+
+
+def tile_picked_kqhopngaplerp_none_po_kernel(
+    tc, x_words, x_scales, w1_words, w1_scales, w2_words, w2_scales, ga, gb,
+    offs, two, n1, n2, n3, n4, n5, n6, n7, out_0, out_1, out_2,
+):
+    nc = tc.nc
+    with ExitStack() as ctx:
+        held = ctx.enter_context(tc.tile_pool(name="held", bufs=1))
+        psum = ctx.enter_context(tc.psum_pool(name="psum", bufs=1))
+
+        def sb(name, shape, dtype):
+            return held.tile(shape, dtype, name=name, align_bytes=64)
+
+        lists = {}
+
+        def load_list(name, dram):
+            lists[name] = held.tile([P, N // 16], U16, name="list_" + name)
+            nc.sync.dma_start(lists[name][:], dram)
+
+        x_s = sb("x_s", [P, T], U8)
+        w_s_raw = sb("w_s_raw", [P, H], U8)
+        nc.vector.memset(x_s[:].bitcast(I32), 0)
+        nc.vector.memset(w_s_raw[:].bitcast(I32), 0)
+
+        x_w = sb("x_w", [P, T], U32)
+        w1_raw = sb("w1_raw", [P, H], I32)
+        w2_raw = sb("w2_raw", [P, H], I32)
+        ga_t = sb("ga_t", [P, PACK], F32)
+        gb_t = sb("gb_t", [P, PACK], F32)
+
+        load_list("offs", offs)
+        load_scale_rows(nc.scalar, x_s, 0, x_scales)
+        load_list("two", two)
+        nc.sync.dma_start(out=w1_raw[:], in_=words_of(w1_words))
+        nc.sync.dma_start(out=x_w[:].bitcast(I32), in_=words_of(x_words))
+        nc.gpsimd.dma_start(out=ga_t[:], in_=ga.rearrange("(p t) o -> p (t o)", t=PACK))
+        nc.gpsimd.dma_start(out=gb_t[:], in_=gb.rearrange("(p t) o -> p (t o)", t=PACK))
+        load_scale_rows(nc.sync, w_s_raw, 0, w1_scales)
+        load_scale_rows(nc.sync, w_s_raw, 4, w2_scales)
+        load_list("n1", n1)
+        nc.sync.dma_start(out=w2_raw[:], in_=words_of(w2_words))
+        for name, dram in (("n4", n4), ("n3", n3), ("n2", n2), ("n6", n6), ("n7", n7), ("n5", n5)):
+            load_list(name, dram)
+
+        warm = sb("warm", [P, 2], F32)
+        nc.vector.memset(warm[:, 0:1], 1.0)
+        nc.scalar.activation(warm[:, 1:2], warm[:, 0:1], ACT.Ln)
+
+        xa_s = sb("xa_s", [P, S], U8)
+        xb_s = sb("xb_s", [P, V], U8)
+        xa_w = sb("xa_w", [P, S], U32)
+        xb_w = sb("xb_w", [P, V], U32)
+        w1_d = sb("w1_d", [P, H], I32)
+        w2_d = sb("w2_d", [P, H], I32)
+        w_s = sb("w_s", [P, H], U8)
+
+        def deal(dst, src):
+            nc.vector.tensor_copy(
+                out=dst[:].rearrange("p (t m) -> p m t", t=PACK),
+                in_=src[:].rearrange("p (m t) -> p m t", t=PACK),
+            )
+
+        nc.vector.tensor_copy(xa_s[:], x_s[:].indirect(lists["offs"][:]))
+        nc.vector.tensor_copy(xb_s[:], x_s[:].indirect(lists["two"][:]))
+        deal(w1_d, w1_raw)
+        nc.vector.tensor_copy(xa_w[:], x_w[:].indirect(lists["offs"][:]))
+        deal(w_s, w_s_raw)
+
+        neg_ga = sb("neg_ga", [P, PACK], F32)
+        abs_ga = sb("abs_ga", [P, PACK], F32)
+        safe_ga = sb("safe_ga", [P, PACK], F32)
+        inv_ga = sb("inv_ga", [P, PACK], F32)
+        nc.vector.tensor_scalar(neg_ga[:], ga_t[:], -1.0, None, ALU.mult)
+        nc.vector.tensor_tensor(abs_ga[:], neg_ga[:], ga_t[:], ALU.max)
+        nc.vector.tensor_scalar(safe_ga[:], abs_ga[:], TINY, None, ALU.max)
+        nc.vector.reciprocal(inv_ga[:], safe_ga[:])
+
+        nc.vector.tensor_copy(xb_w[:], x_w[:].indirect(lists["two"][:]))
+        deal(w2_d, w2_raw)
+
+        def product(bank, t, st_words, st_scales, mv_words, mv_scales):
+            acc = psum.tile([P, N], F32, name="acc", tag="bank%d" % bank)
+            cols = slice(t * P, (t + 1) * P)
+            nc.tensor.matmul_mx(
+                out=acc[:],
+                lhsT=st_words[:, cols].bitcast(FP8X4),
+                lhsT_scale=st_scales[:, cols],
+                rhs=mv_words.bitcast(FP8X4),
+                rhs_scale=mv_scales,
+                start=True,
+                stop=True,
+            )
+            return acc
+
+        a_ps = [product(t, t, w1_d[:], w_s[:], xa_w[:], xa_s[:]) for t in range(PACK)]
+        b_ps = [product(PACK + t, t, w2_d[:], w_s[4:P, :], xb_w[:], xb_s[:]) for t in range(PACK)]
+
+        a_win = [sb("a_win%d" % t, [P, WINDOW], F32) for t in range(PACK)]
+        b_win = [sb("b_win%d" % t, [P, WINDOW], F32) for t in range(PACK)]
+        l_win = [sb("l_win%d" % t, [P, WINDOW], F32) for t in range(PACK)]
+        a_copy = [sb("a_copy%d" % t, [P, N], F32) for t in range(PACK)]
+        b_n4 = [sb("b_n4%d" % t, [P, N], F32) for t in range(PACK)]
+        num = sb("num", [P, PACK, N], F32)
+        rec = sb("rec", [P, PACK, N], F32)
+        z2 = sb("z2", [P, PACK, N], F32)
+
+        for t in range(PACK):
+            nc.scalar.activation(a_win[t][:, 0:N], a_ps[t][:], ACT.Copy, scale=neg_ga[:, t : t + 1])
+        for t in range(PACK):
+            nc.vector.tensor_copy(a_copy[t][:], a_win[t][:, 0:N])
+            nc.vector.tensor_tensor(num[:, t, :], a_win[t][:].indirect(lists["n1"][:]), a_copy[t][:], ALU.subtract)
+        for t in range(PACK):
+            nc.scalar.activation(l_win[t][:, N:WINDOW], num[:, t, :], ACT.Abs, scale=inv_ga[:, t : t + 1])
+            nc.scalar.activation(l_win[t][:, 0:N], l_win[t][:, N:WINDOW], ACT.Ln, bias=0.5)
+            nc.scalar.activation(b_win[t][:, 0:N], b_ps[t][:], ACT.Copy, scale=gb_t[:, t : t + 1])
+        for t in range(PACK):
+            nc.vector.tensor_copy(b_n4[t][:], b_win[t][:].indirect(lists["n4"][:]))
+            nc.vector.tensor_tensor(z2[:, t, :], b_win[t][:].indirect(lists["n3"][:]), b_n4[t][:], ALU.subtract)
+        for t in range(PACK):
+            nc.scalar.activation(rec[:, t, :], l_win[t][:].indirect(lists["n2"][:]), ACT.Exp, scale=-1.0)
+
+        warm2 = sb("warm2", [P, 1], F32)
+        nc.scalar.activation(warm2[:], rec[:, PACK - 1, 0:1], ACT.Sigmoid)
+
+        z_bf = sb("z_bf", [P, PACK * N], BF16)
+        z2_bf = sb("z2_bf", [P, PACK * N], BF16)
+        nc.vector.tensor_tensor(
+            z_bf[:].rearrange("p (u m k) -> p m k u", u=PACK, k=PACK),
+            num[:].rearrange("p k (m u) -> p m k u", u=PACK),
+            rec[:].rearrange("p k (m u) -> p m k u", u=PACK),
+            ALU.mult,
+        )
+
+        def interleave(dst, src, copy=nc.scalar.copy):
+            copy(
+                out=dst.rearrange("p (c i k) -> p c k i", i=4, k=PACK),
+                in_=src.rearrange("p k (c i) -> p c k i", i=4),
+            )
+
+        interleave(z2_bf[:], z2[:])
+        z_w = sb("z_w", [P, N], U32)
+        z_s = sb("z_s", [P, N], U8)
+        z2_w = sb("z2_w", [P, N], U32)
+        z2_s = sb("z2_s", [P, N], U8)
+        nc.vector.quantize_mx(out=z_w[:].bitcast(FP8X4), scales=z_s[:], in_=z_bf[:])
+        nc.vector.quantize_mx(out=z2_w[:].bitcast(FP8X4), scales=z2_s[:], in_=z2_bf[:])
+
+        s_ps = [product(t, t, z_w[:], z_s[:], z2_w[:], z2_s[:]) for t in range(PACK)]
+        s_win = [sb("s_win%d" % t, [P, WINDOW], F32) for t in range(PACK)]
+
+        o_w = sb("o_w", [P, N], U32)
+        o_s = sb("o_s", [P, N], U8)
+        out_rows = out_0.rearrange("(p t) v -> p t v", t=PACK)
+        out_words = words_of(out_1)
+        for h in range(2):
+            cols = slice(h * HALF, (h + 1) * HALF)
+            entries = slice(h * HALF // 16, (h + 1) * HALF // 16)
+            res = sb("res%d" % h, [P, PACK, HALF], F32)
+            for t in range(PACK):
+                if h == 0:
+                    nc.scalar.activation(s_win[t][:, 0:N], s_ps[t][:], ACT.Copy, scale=0.0625)
+                gate = sb("gate%d_%d" % (h, t), [P, HALF], F32)
+                rest = sb("rest%d_%d" % (h, t), [P, HALF], F32)
+                far = sb("far%d_%d" % (h, t), [P, HALF], F32)
+                near = sb("near%d_%d" % (h, t), [P, HALF], F32)
+                nc.scalar.activation(gate[:], s_win[t][:].indirect(lists["n6"][:, entries]), ACT.Sigmoid)
+                if h == 0 and t == 0:
+                    nc.vector.tensor_copy(near[:], s_win[t][:].indirect(lists["n5"][:, entries]))
+                    nc.vector.tensor_tensor(rest[:], s_win[t][:].indirect(lists["n7"][:, entries]), near[:], ALU.subtract)
+                    nc.vector.tensor_tensor(far[:], rest[:], gate[:], ALU.mult)
+                else:
+                    nc.scalar.activation(rest[:], gate[:], ACT.Copy, scale=-1.0, bias=1.0)
+                    nc.vector.tensor_tensor(far[:], s_win[t][:].indirect(lists["n7"][:, entries]), gate[:], ALU.mult)
+                    nc.vector.tensor_tensor(near[:], s_win[t][:].indirect(lists["n5"][:, entries]), rest[:], ALU.mult)
+                nc.vector.tensor_tensor(res[:, t, :], far[:], near[:], ALU.add)
+                nc.sync.dma_start(out=out_rows[:, t, cols], in_=res[:, t, :])
+            o_bf = sb("o_bf%d" % h, [P, PACK * HALF], BF16)
+            interleave(o_bf[:], res[:], nc.scalar.copy if h == 0 else nc.vector.tensor_copy)
+            nc.vector.quantize_mx(out=o_w[:, cols].bitcast(FP8X4), scales=o_s[:, cols], in_=o_bf[:])
+            nc.sync.dma_start(out=out_words[:, cols], in_=o_w[:, cols].bitcast(I32))
+        for q in range(4):
+            queue = nc.sync if q % 2 == 0 else nc.scalar
+            queue.dma_start(
+                out=out_2[0, 4 * q : 4 * q + 4, :].bitcast(I32),
+                in_=o_s[32 * q : 32 * q + 4, :].bitcast(I32),
+            )

@@ -1,6 +1,7 @@
 from contextlib import ExitStack
 
 import concourse.mybir as mybir
+from concourse.masks import make_identity
 
 K, T, S, V, H = 512, 2048, 512, 512, 512
 FLOPS = 2 * K * H * S + 2 * K * H * V + 2 * H * S * V
@@ -23,10 +24,10 @@ HALF = N // 2
 TINY = 1e-37
 
 
-def load_scale_rows(queue, tile, first, scales):
+def load_scale_rows(queues, tile, scales):
     for q in range(4):
-        queue.dma_start(
-            out=tile[32 * q + first : 32 * q + first + 4, :].bitcast(I32),
+        queues[q % len(queues)].dma_start(
+            out=tile[32 * q : 32 * q + 4, :].bitcast(I32),
             in_=scales[0, 4 * q : 4 * q + 4, :].bitcast(I32),
         )
 
@@ -44,8 +45,8 @@ def tile_picked_kqhopngaplerp_none_po_kernel(
         held = ctx.enter_context(tc.tile_pool(name="held", bufs=1))
         psum = ctx.enter_context(tc.psum_pool(name="psum", bufs=1))
 
-        def sb(name, shape, dtype):
-            return held.tile(shape, dtype, name=name, align_bytes=64)
+        def sb(name, shape, dtype, tag=""):
+            return held.tile(shape, dtype, name=name, tag=tag or name, align_bytes=64)
 
         lists = {}
 
@@ -54,27 +55,41 @@ def tile_picked_kqhopngaplerp_none_po_kernel(
             nc.sync.dma_start(lists[name][:], dram)
 
         x_s = sb("x_s", [P, T], U8)
-        w_s_raw = sb("w_s_raw", [P, H], U8)
-        nc.vector.memset(x_s[:].bitcast(I32), 0)
-        nc.vector.memset(w_s_raw[:].bitcast(I32), 0)
-
+        w1_s_raw = sb("w1_s_raw", [P, H], U8)
+        w2_s_raw = sb("w2_s_raw", [P, H], U8)
         x_w = sb("x_w", [P, T], U32)
         w1_raw = sb("w1_raw", [P, H], I32)
         w2_raw = sb("w2_raw", [P, H], I32)
-        ga_t = sb("ga_t", [P, PACK], F32)
-        gb_t = sb("gb_t", [P, PACK], F32)
+        ga_rows = sb("ga_rows", [P, P], F32)
+        gb_rows = sb("gb_rows", [P, P], F32)
+        identity = sb("identity", [P, P], F32)
+        for plane in (x_s, w1_s_raw, w2_s_raw):
+            nc.vector.memset(plane[:].bitcast(I32), 0)
 
+        def load_gain(rows, dram):
+            nc.gpsimd.memset(rows[:], 0.0)
+            nc.gpsimd.dma_start(
+                out=rows[0:PACK, :].rearrange("t (q r) -> t q r", r=8),
+                in_=dram.rearrange("(q t r) o -> t q (r o)", t=PACK, r=8),
+            )
+
+        def turn_gain(name, rows, bank):
+            turned = psum.tile([P, N], F32, name=name, tag="bank%d" % bank)
+            nc.tensor.transpose(turned[:, 0:P], rows[:], identity[:])
+            return turned[:, 0:PACK]
+
+        load_gain(ga_rows, ga)
+        make_identity(nc, identity[:])
+        load_gain(gb_rows, gb)
         load_list("offs", offs)
-        load_scale_rows(nc.scalar, x_s, 0, x_scales)
         load_list("two", two)
-        nc.sync.dma_start(out=w1_raw[:], in_=words_of(w1_words))
-        nc.sync.dma_start(out=x_w[:].bitcast(I32), in_=words_of(x_words))
-        nc.gpsimd.dma_start(out=ga_t[:], in_=ga.rearrange("(p t) o -> p (t o)", t=PACK))
-        nc.gpsimd.dma_start(out=gb_t[:], in_=gb.rearrange("(p t) o -> p (t o)", t=PACK))
-        load_scale_rows(nc.sync, w_s_raw, 0, w1_scales)
-        load_scale_rows(nc.sync, w_s_raw, 4, w2_scales)
         load_list("n1", n1)
+        load_scale_rows((nc.sync, nc.scalar), x_s, x_scales)
+        nc.sync.dma_start(out=x_w[:].bitcast(I32), in_=words_of(x_words))
+        nc.sync.dma_start(out=w1_raw[:], in_=words_of(w1_words))
+        load_scale_rows((nc.sync,), w1_s_raw, w1_scales)
         nc.sync.dma_start(out=w2_raw[:], in_=words_of(w2_words))
+        load_scale_rows((nc.sync,), w2_s_raw, w2_scales)
         for name, dram in (("n4", n4), ("n3", n3), ("n2", n2), ("n6", n6), ("n7", n7), ("n5", n5)):
             load_list(name, dram)
 
@@ -85,34 +100,39 @@ def tile_picked_kqhopngaplerp_none_po_kernel(
         xa_s = sb("xa_s", [P, S], U8)
         xb_s = sb("xb_s", [P, V], U8)
         xa_w = sb("xa_w", [P, S], U32)
-        xb_w = sb("xb_w", [P, V], U32)
         w1_d = sb("w1_d", [P, H], I32)
         w2_d = sb("w2_d", [P, H], I32)
-        w_s = sb("w_s", [P, H], U8)
+        w1_s = sb("w1_s", [P, H], U8)
+        w2_s = sb("w2_s", [P, H], U8)
 
         def deal(dst, src):
-            nc.vector.tensor_copy(
-                out=dst[:].rearrange("p (t m) -> p m t", t=PACK),
-                in_=src[:].rearrange("p (m t) -> p m t", t=PACK),
+            nc.gpsimd.tensor_copy(
+                out=dst[:].bitcast(I32).rearrange("p (t q i) -> p t q i", t=PACK, q=16),
+                in_=src[:].bitcast(I32).rearrange("p (q t i) -> p t q i", t=PACK, q=16),
             )
+
+        ga_ps = turn_gain("ga_ps", ga_rows, 6)
+        gb_ps = turn_gain("gb_ps", gb_rows, 7)
+        neg_ga, abs_ga, safe_ga, inv_ga, gb_t = [
+            sb(name, [P, PACK], F32) for name in ("neg_ga", "abs_ga", "safe_ga", "inv_ga", "gb_t")
+        ]
+        nc.scalar.activation(neg_ga[:], ga_ps, ACT.Copy, scale=-1.0)
+        nc.scalar.activation(abs_ga[:], ga_ps, ACT.Abs)
+        nc.scalar.copy(gb_t[:], gb_ps)
 
         nc.vector.tensor_copy(xa_s[:], x_s[:].indirect(lists["offs"][:]))
         nc.vector.tensor_copy(xb_s[:], x_s[:].indirect(lists["two"][:]))
-        deal(w1_d, w1_raw)
         nc.vector.tensor_copy(xa_w[:], x_w[:].indirect(lists["offs"][:]))
-        deal(w_s, w_s_raw)
+        deal(w1_d, w1_raw)
+        deal(w1_s, w1_s_raw)
 
-        neg_ga = sb("neg_ga", [P, PACK], F32)
-        abs_ga = sb("abs_ga", [P, PACK], F32)
-        safe_ga = sb("safe_ga", [P, PACK], F32)
-        inv_ga = sb("inv_ga", [P, PACK], F32)
-        nc.vector.tensor_scalar(neg_ga[:], ga_t[:], -1.0, None, ALU.mult)
-        nc.vector.tensor_tensor(abs_ga[:], neg_ga[:], ga_t[:], ALU.max)
-        nc.vector.tensor_scalar(safe_ga[:], abs_ga[:], TINY, None, ALU.max)
-        nc.vector.reciprocal(inv_ga[:], safe_ga[:])
-
+        xb_w = sb("xb_w", [P, V], U32)
         nc.vector.tensor_copy(xb_w[:], x_w[:].indirect(lists["two"][:]))
         deal(w2_d, w2_raw)
+        deal(w2_s, w2_s_raw)
+
+        nc.vector.tensor_scalar(safe_ga[:], abs_ga[:], TINY, None, ALU.max)
+        nc.vector.reciprocal(inv_ga[:], safe_ga[:])
 
         def product(bank, t, st_words, st_scales, mv_words, mv_scales):
             acc = psum.tile([P, N], F32, name="acc", tag="bank%d" % bank)
@@ -128,37 +148,42 @@ def tile_picked_kqhopngaplerp_none_po_kernel(
             )
             return acc
 
-        a_ps = [product(t, t, w1_d[:], w_s[:], xa_w[:], xa_s[:]) for t in range(PACK)]
-        b_ps = [product(PACK + t, t, w2_d[:], w_s[4:P, :], xb_w[:], xb_s[:]) for t in range(PACK)]
+        a_ps = [product(t, t, w1_d[:], w1_s[:], xa_w[:], xa_s[:]) for t in range(PACK)]
+        b_ps = [product(PACK + t, t, w2_d[:], w2_s[:], xb_w[:], xb_s[:]) for t in range(PACK)]
 
         a_win = [sb("a_win%d" % t, [P, WINDOW], F32) for t in range(PACK)]
         b_win = [sb("b_win%d" % t, [P, WINDOW], F32) for t in range(PACK)]
         l_win = [sb("l_win%d" % t, [P, WINDOW], F32) for t in range(PACK)]
         a_copy = [sb("a_copy%d" % t, [P, N], F32) for t in range(PACK)]
-        b_n4 = [sb("b_n4%d" % t, [P, N], F32) for t in range(PACK)]
+        b_n4 = [sb("b_n4%d" % t, [P, N], F32, tag=("a_copy3", "a_win3")[t % 2]) for t in range(PACK)]
+        size = [sb("size%d" % t, [P, N], F32) for t in range(PACK)]
         num = sb("num", [P, PACK, N], F32)
-        rec = sb("rec", [P, PACK, N], F32)
+        rec = sb("rec", [P, PACK, N], F32, tag="size3")
         z2 = sb("z2", [P, PACK, N], F32)
 
         for t in range(PACK):
             nc.scalar.activation(a_win[t][:, 0:N], a_ps[t][:], ACT.Copy, scale=neg_ga[:, t : t + 1])
         for t in range(PACK):
-            nc.vector.tensor_copy(a_copy[t][:], a_win[t][:, 0:N])
+            if t < 2:
+                nc.vector.tensor_copy(a_copy[t][:], a_win[t][:, 0:N])
+            else:
+                nc.sync.dma_start(out=a_copy[t][:], in_=a_win[t][:, 0:N])
             nc.vector.tensor_tensor(num[:, t, :], a_win[t][:].indirect(lists["n1"][:]), a_copy[t][:], ALU.subtract)
         for t in range(PACK):
-            nc.scalar.activation(l_win[t][:, N:WINDOW], num[:, t, :], ACT.Abs, scale=inv_ga[:, t : t + 1])
-            nc.scalar.activation(l_win[t][:, 0:N], l_win[t][:, N:WINDOW], ACT.Ln, bias=0.5)
+            nc.scalar.activation(size[t][:], num[:, t, :], ACT.Abs, scale=inv_ga[:, t : t + 1])
+            nc.scalar.activation(l_win[t][:, 0:N], size[t][:], ACT.Ln, bias=0.5)
             nc.scalar.activation(b_win[t][:, 0:N], b_ps[t][:], ACT.Copy, scale=gb_t[:, t : t + 1])
-        for t in range(PACK):
-            nc.vector.tensor_copy(b_n4[t][:], b_win[t][:].indirect(lists["n4"][:]))
-            nc.vector.tensor_tensor(z2[:, t, :], b_win[t][:].indirect(lists["n3"][:]), b_n4[t][:], ALU.subtract)
+        for t in range(PACK + 1):
+            if t < PACK:
+                nc.vector.tensor_copy(b_n4[t][:], b_win[t][:].indirect(lists["n4"][:]))
+            if t > 0:
+                nc.vector.tensor_tensor(
+                    z2[:, t - 1, :], b_win[t - 1][:].indirect(lists["n3"][:]), b_n4[t - 1][:], ALU.subtract
+                )
         for t in range(PACK):
             nc.scalar.activation(rec[:, t, :], l_win[t][:].indirect(lists["n2"][:]), ACT.Exp, scale=-1.0)
 
-        warm2 = sb("warm2", [P, 1], F32)
-        nc.scalar.activation(warm2[:], rec[:, PACK - 1, 0:1], ACT.Sigmoid)
-
-        z_bf = sb("z_bf", [P, PACK * N], BF16)
+        z_bf = sb("z_bf", [P, PACK * N], BF16, tag="a_win3")
         z2_bf = sb("z2_bf", [P, PACK * N], BF16)
         nc.vector.tensor_tensor(
             z_bf[:].rearrange("p (u m k) -> p m k u", u=PACK, k=PACK),
@@ -174,12 +199,19 @@ def tile_picked_kqhopngaplerp_none_po_kernel(
             )
 
         interleave(z2_bf[:], z2[:])
+        warm2 = sb("warm2", [P, 1], F32)
+        nc.scalar.activation(warm2[:], z2_bf[:, 0:1], ACT.Sigmoid)
         z_w = sb("z_w", [P, N], U32)
         z_s = sb("z_s", [P, N], U8)
         z2_w = sb("z2_w", [P, N], U32)
         z2_s = sb("z2_s", [P, N], U8)
-        nc.vector.quantize_mx(out=z_w[:].bitcast(FP8X4), scales=z_s[:], in_=z_bf[:])
-        nc.vector.quantize_mx(out=z2_w[:].bitcast(FP8X4), scales=z2_s[:], in_=z2_bf[:])
+        for t in range(PACK):
+            cols = slice(t * P, (t + 1) * P)
+            nc.vector.quantize_mx(
+                out=z_w[:, cols].bitcast(FP8X4), scales=z_s[:, cols], in_=z_bf[:, t * N : (t + 1) * N]
+            )
+            if t == 0:
+                nc.vector.quantize_mx(out=z2_w[:].bitcast(FP8X4), scales=z2_s[:], in_=z2_bf[:])
 
         s_ps = [product(t, t, z_w[:], z_s[:], z2_w[:], z2_s[:]) for t in range(PACK)]
         s_win = [sb("s_win%d" % t, [P, WINDOW], F32) for t in range(PACK)]
@@ -188,32 +220,39 @@ def tile_picked_kqhopngaplerp_none_po_kernel(
         o_s = sb("o_s", [P, N], U8)
         out_rows = out_0.rearrange("(p t) v -> p t v", t=PACK)
         out_words = words_of(out_1)
-        for h in range(2):
-            cols = slice(h * HALF, (h + 1) * HALF)
-            entries = slice(h * HALF // 16, (h + 1) * HALF // 16)
-            res = sb("res%d" % h, [P, PACK, HALF], F32)
-            for t in range(PACK):
-                if h == 0:
-                    nc.scalar.activation(s_win[t][:, 0:N], s_ps[t][:], ACT.Copy, scale=0.0625)
-                gate = sb("gate%d_%d" % (h, t), [P, HALF], F32)
-                rest = sb("rest%d_%d" % (h, t), [P, HALF], F32)
-                far = sb("far%d_%d" % (h, t), [P, HALF], F32)
-                near = sb("near%d_%d" % (h, t), [P, HALF], F32)
-                nc.scalar.activation(gate[:], s_win[t][:].indirect(lists["n6"][:, entries]), ACT.Sigmoid)
-                if h == 0 and t == 0:
-                    nc.vector.tensor_copy(near[:], s_win[t][:].indirect(lists["n5"][:, entries]))
-                    nc.vector.tensor_tensor(rest[:], s_win[t][:].indirect(lists["n7"][:, entries]), near[:], ALU.subtract)
-                    nc.vector.tensor_tensor(far[:], rest[:], gate[:], ALU.mult)
-                else:
-                    nc.scalar.activation(rest[:], gate[:], ACT.Copy, scale=-1.0, bias=1.0)
-                    nc.vector.tensor_tensor(far[:], s_win[t][:].indirect(lists["n7"][:, entries]), gate[:], ALU.mult)
-                    nc.vector.tensor_tensor(near[:], s_win[t][:].indirect(lists["n5"][:, entries]), rest[:], ALU.mult)
-                nc.vector.tensor_tensor(res[:, t, :], far[:], near[:], ALU.add)
-                nc.sync.dma_start(out=out_rows[:, t, cols], in_=res[:, t, :])
-            o_bf = sb("o_bf%d" % h, [P, PACK * HALF], BF16)
-            interleave(o_bf[:], res[:], nc.scalar.copy if h == 0 else nc.vector.tensor_copy)
+        res = sb("res", [P, PACK, N], F32)
+
+        def blend(t, first, last):
+            cols = slice(first, last)
+            entries = slice(first // 16, last // 16)
+            gate, rest, far, near = [sb("%s%d_%d" % (n, t, first), [P, last - first], F32) for n in ("gate", "rest", "far", "near")]
+            nc.scalar.activation(gate[:], s_win[t][:].indirect(lists["n6"][:, entries]), ACT.Sigmoid)
+            if t == 0:
+                nc.vector.tensor_copy(near[:], s_win[t][:].indirect(lists["n5"][:, entries]))
+                nc.vector.tensor_tensor(rest[:], s_win[t][:].indirect(lists["n7"][:, entries]), near[:], ALU.subtract)
+                nc.vector.tensor_tensor(far[:], rest[:], gate[:], ALU.mult)
+            else:
+                nc.scalar.activation(rest[:], gate[:], ACT.Copy, scale=-1.0, bias=1.0)
+                nc.vector.tensor_tensor(far[:], s_win[t][:].indirect(lists["n7"][:, entries]), gate[:], ALU.mult)
+                nc.vector.tensor_tensor(near[:], s_win[t][:].indirect(lists["n5"][:, entries]), rest[:], ALU.mult)
+            nc.vector.tensor_tensor(res[:, t, cols], far[:], near[:], ALU.add)
+            nc.sync.dma_start(out=out_rows[:, t, cols], in_=res[:, t, cols])
+
+        def hand_on(first, last, copy):
+            cols = slice(first, last)
+            o_bf = sb("o_bf%d" % first, [P, PACK * (last - first)], BF16)
+            interleave(o_bf[:], res[:, :, cols], copy)
             nc.vector.quantize_mx(out=o_w[:, cols].bitcast(FP8X4), scales=o_s[:, cols], in_=o_bf[:])
             nc.sync.dma_start(out=out_words[:, cols], in_=o_w[:, cols].bitcast(I32))
+
+        for t in range(PACK):
+            nc.scalar.activation(s_win[t][:, 0:N], s_ps[t][:], ACT.Copy, scale=0.0625)
+            if t < PACK - 1:
+                blend(t, 0, N)
+        blend(PACK - 1, 0, HALF)
+        blend(PACK - 1, HALF, N)
+        hand_on(0, HALF, nc.scalar.copy)
+        hand_on(HALF, N, nc.vector.tensor_copy)
         for q in range(4):
             queue = nc.sync if q % 2 == 0 else nc.scalar
             queue.dma_start(

@@ -83,11 +83,11 @@ def tile_picked_kqhopngaplerp_none_po_kernel(
         load_gain(gb_rows, gb)
         load_list("offs", offs)
         load_list("two", two)
-        load_list("n1", n1)
-        load_scale_rows((nc.sync, nc.scalar), x_s, x_scales)
-        nc.sync.dma_start(out=x_w[:].bitcast(I32), in_=words_of(x_words))
         nc.sync.dma_start(out=w1_raw[:], in_=words_of(w1_words))
+        load_scale_rows((nc.sync,), x_s, x_scales)
+        nc.sync.dma_start(out=x_w[:].bitcast(I32), in_=words_of(x_words))
         load_scale_rows((nc.sync,), w1_s_raw, w1_scales)
+        load_list("n1", n1)
         nc.sync.dma_start(out=w2_raw[:], in_=words_of(w2_words))
         load_scale_rows((nc.sync,), w2_s_raw, w2_scales)
         for name, dram in (("n4", n4), ("n3", n3), ("n2", n2), ("n6", n6), ("n7", n7), ("n5", n5)):
@@ -135,10 +135,11 @@ def tile_picked_kqhopngaplerp_none_po_kernel(
         nc.vector.reciprocal(inv_ga[:], safe_ga[:])
 
         def product(bank, t, st_words, st_scales, mv_words, mv_scales):
-            acc = psum.tile([P, N], F32, name="acc", tag="bank%d" % bank)
+            whole = psum.tile([P, N], F32, name="acc", tag="bank%d" % bank)
+            acc = whole[:, 0 : mv_words.shape[1]]
             cols = slice(t * P, (t + 1) * P)
             nc.tensor.matmul_mx(
-                out=acc[:],
+                out=acc,
                 lhsT=st_words[:, cols].bitcast(FP8X4),
                 lhsT_scale=st_scales[:, cols],
                 rhs=mv_words.bitcast(FP8X4),
@@ -156,13 +157,13 @@ def tile_picked_kqhopngaplerp_none_po_kernel(
         l_win = [sb("l_win%d" % t, [P, WINDOW], F32) for t in range(PACK)]
         a_copy = [sb("a_copy%d" % t, [P, N], F32) for t in range(PACK)]
         b_n4 = [sb("b_n4%d" % t, [P, N], F32, tag=("a_copy3", "a_win3")[t % 2]) for t in range(PACK)]
-        size = [sb("size%d" % t, [P, N], F32) for t in range(PACK)]
+        size = [sb("size%d" % t, [P, N], F32, tag="neg_ga" if t == 0 else "") for t in range(PACK)]
         num = sb("num", [P, PACK, N], F32)
         rec = sb("rec", [P, PACK, N], F32, tag="size3")
         z2 = sb("z2", [P, PACK, N], F32)
 
         for t in range(PACK):
-            nc.scalar.activation(a_win[t][:, 0:N], a_ps[t][:], ACT.Copy, scale=neg_ga[:, t : t + 1])
+            nc.scalar.activation(a_win[t][:, 0:N], a_ps[t], ACT.Copy, scale=neg_ga[:, t : t + 1])
         for t in range(PACK):
             if t < 2:
                 nc.vector.tensor_copy(a_copy[t][:], a_win[t][:, 0:N])
@@ -172,7 +173,7 @@ def tile_picked_kqhopngaplerp_none_po_kernel(
         for t in range(PACK):
             nc.scalar.activation(size[t][:], num[:, t, :], ACT.Abs, scale=inv_ga[:, t : t + 1])
             nc.scalar.activation(l_win[t][:, 0:N], size[t][:], ACT.Ln, bias=0.5)
-            nc.scalar.activation(b_win[t][:, 0:N], b_ps[t][:], ACT.Copy, scale=gb_t[:, t : t + 1])
+            nc.scalar.activation(b_win[t][:, 0:N], b_ps[t], ACT.Copy, scale=gb_t[:, t : t + 1])
         for t in range(PACK + 1):
             if t < PACK:
                 nc.vector.tensor_copy(b_n4[t][:], b_win[t][:].indirect(lists["n4"][:]))
@@ -198,23 +199,34 @@ def tile_picked_kqhopngaplerp_none_po_kernel(
                 in_=src.rearrange("p k (c i) -> p c k i", i=4),
             )
 
-        interleave(z2_bf[:], z2[:])
+        halves = (slice(0, HALF), slice(HALF, N))
+        for cols in halves:
+            interleave(z2_bf[:, PACK * cols.start : PACK * cols.stop], z2[:, :, cols])
         warm2 = sb("warm2", [P, 1], F32)
-        nc.scalar.activation(warm2[:], z2_bf[:, 0:1], ACT.Sigmoid)
+        nc.scalar.activation(warm2[:], z2_bf[:, PACK * N - 1 : PACK * N], ACT.Sigmoid)
         z_w = sb("z_w", [P, N], U32)
         z_s = sb("z_s", [P, N], U8)
         z2_w = sb("z2_w", [P, N], U32)
         z2_s = sb("z2_s", [P, N], U8)
-        for t in range(PACK):
-            cols = slice(t * P, (t + 1) * P)
-            nc.vector.quantize_mx(
-                out=z_w[:, cols].bitcast(FP8X4), scales=z_s[:, cols], in_=z_bf[:, t * N : (t + 1) * N]
-            )
-            if t == 0:
-                nc.vector.quantize_mx(out=z2_w[:].bitcast(FP8X4), scales=z2_s[:], in_=z2_bf[:])
 
-        s_ps = [product(t, t, z_w[:], z_s[:], z2_w[:], z2_s[:]) for t in range(PACK)]
+        def quantize(words, scales, values, cols):
+            nc.vector.quantize_mx(
+                out=words[:, cols].bitcast(FP8X4),
+                scales=scales[:, cols],
+                in_=values[:, PACK * cols.start : PACK * cols.stop],
+            )
+
+        quantize(z2_w, z2_s, z2_bf, halves[0])
+        quantize(z_w, z_s, z_bf, slice(0, P))
+        quantize(z2_w, z2_s, z2_bf, halves[1])
+        for t in range(1, PACK):
+            quantize(z_w, z_s, z_bf, slice(t * P, (t + 1) * P))
+
         s_win = [sb("s_win%d" % t, [P, WINDOW], F32) for t in range(PACK)]
+        s_first = [product(PACK + h, 0, z_w[:], z_s[:], z2_w[:, cols], z2_s[:, cols]) for h, cols in enumerate(halves)]
+        s_ps = [None] + [product(t, t, z_w[:], z_s[:], z2_w[:], z2_s[:]) for t in range(1, PACK)]
+        for h, cols in enumerate(halves):
+            nc.vector.tensor_scalar(s_win[0][:, cols], s_first[h], 0.0625, None, ALU.mult)
 
         o_w = sb("o_w", [P, N], U32)
         o_s = sb("o_s", [P, N], U8)
@@ -246,7 +258,8 @@ def tile_picked_kqhopngaplerp_none_po_kernel(
             nc.sync.dma_start(out=out_words[:, cols], in_=o_w[:, cols].bitcast(I32))
 
         for t in range(PACK):
-            nc.scalar.activation(s_win[t][:, 0:N], s_ps[t][:], ACT.Copy, scale=0.0625)
+            if t > 0:
+                nc.scalar.activation(s_win[t][:, 0:N], s_ps[t], ACT.Copy, scale=0.0625)
             if t < PACK - 1:
                 blend(t, 0, N)
         blend(PACK - 1, 0, HALF)

@@ -58,7 +58,6 @@ def tile_picked_kqhopngaplerp_none_po_kernel(
         w1_s_raw = sb("w1_s_raw", [P, H], U8)
         w2_s_raw = sb("w2_s_raw", [P, H], U8)
         x_w = sb("x_w", [P, T], U32)
-        w1_raw = sb("w1_raw", [P, H], I32)
         w2_raw = sb("w2_raw", [P, H], I32)
         ga_rows = sb("ga_rows", [P, P], F32)
         gb_rows = sb("gb_rows", [P, P], F32)
@@ -83,19 +82,20 @@ def tile_picked_kqhopngaplerp_none_po_kernel(
         load_gain(gb_rows, gb)
         load_list("offs", offs)
         load_list("two", two)
-        nc.sync.dma_start(out=w1_raw[:], in_=words_of(w1_words))
-        load_scale_rows((nc.sync,), x_s, x_scales)
-        nc.sync.dma_start(out=x_w[:].bitcast(I32), in_=words_of(x_words))
-        load_scale_rows((nc.sync,), w1_s_raw, w1_scales)
         load_list("n1", n1)
+        load_scale_rows((nc.sync, nc.scalar), x_s, x_scales)
+        nc.sync.dma_start(out=x_w[:].bitcast(I32), in_=words_of(x_words))
+        warm = sb("warm", [P, 1], F32)
+        warm_out = sb("warm_out", [P, 1], F32)
+        nc.vector.memset(warm[:], 1.0)
+        nc.scalar.activation(warm_out[:], warm[:], ACT.Ln)
+        w1_raw = sb("w1_raw", [P, H], I32, tag="warm")
+        nc.scalar.dma_start(out=w1_raw[:], in_=words_of(w1_words))
+        load_scale_rows((nc.sync,), w1_s_raw, w1_scales)
         nc.sync.dma_start(out=w2_raw[:], in_=words_of(w2_words))
         load_scale_rows((nc.sync,), w2_s_raw, w2_scales)
         for name, dram in (("n4", n4), ("n3", n3), ("n2", n2), ("n6", n6), ("n7", n7), ("n5", n5)):
             load_list(name, dram)
-
-        warm = sb("warm", [P, 2], F32)
-        nc.vector.memset(warm[:, 0:1], 1.0)
-        nc.scalar.activation(warm[:, 1:2], warm[:, 0:1], ACT.Ln)
 
         xa_s = sb("xa_s", [P, S], U8)
         xb_s = sb("xb_s", [P, V], U8)
@@ -105,8 +105,8 @@ def tile_picked_kqhopngaplerp_none_po_kernel(
         w1_s = sb("w1_s", [P, H], U8)
         w2_s = sb("w2_s", [P, H], U8)
 
-        def deal(dst, src):
-            nc.gpsimd.tensor_copy(
+        def deal(dst, src, engine=nc.gpsimd):
+            engine.tensor_copy(
                 out=dst[:].bitcast(I32).rearrange("p (t q i) -> p t q i", t=PACK, q=16),
                 in_=src[:].bitcast(I32).rearrange("p (q t i) -> p t q i", t=PACK, q=16),
             )
@@ -128,7 +128,7 @@ def tile_picked_kqhopngaplerp_none_po_kernel(
 
         xb_w = sb("xb_w", [P, V], U32)
         nc.vector.tensor_copy(xb_w[:], x_w[:].indirect(lists["two"][:]))
-        deal(w2_d, w2_raw)
+        deal(w2_d, w2_raw, nc.vector)
         deal(w2_s, w2_s_raw)
 
         nc.vector.tensor_scalar(safe_ga[:], abs_ga[:], TINY, None, ALU.max)

from contextlib import ExitStack

import concourse.mybir as mybir
from concourse.masks import make_identity

K, T, S, V, H = 512, 2048, 512, 512, 512
FLOPS = 2 * K * H * S + 2 * K * H * V + 2 * H * S * V

F32 = mybir.dt.float32
BF16 = mybir.dt.bfloat16
I32 = mybir.dt.int32
U32 = mybir.dt.uint32
U16 = mybir.dt.uint16
U8 = mybir.dt.uint8
FP8X4 = mybir.dt.float8_e4m3fn_x4
ALU = mybir.AluOpType
ACT = mybir.ActivationFunctionType

P = 128
PACK = 4
N = 512
WINDOW = 2 * N
HALF = N // 2
TINY = 1e-37


def load_scale_rows(queues, tile, scales):
    for q in range(4):
        queues[q % len(queues)].dma_start(
            out=tile[32 * q : 32 * q + 4, :].bitcast(I32),
            in_=scales[0, 4 * q : 4 * q + 4, :].bitcast(I32),
        )


def words_of(dram):
    return dram[0].rearrange("p n t -> p (n t)").bitcast(I32)


def tile_picked_kqhopngaplerp_none_po_kernel(
    tc, x_words, x_scales, w1_words, w1_scales, w2_words, w2_scales, ga, gb,
    offs, two, n1, n2, n3, n4, n5, n6, n7, out_0, out_1, out_2,
):
    nc = tc.nc
    with ExitStack() as ctx:
        held = ctx.enter_context(tc.tile_pool(name="held", bufs=1))
        psum = ctx.enter_context(tc.psum_pool(name="psum", bufs=1))

        def sb(name, shape, dtype, tag=""):
            return held.tile(shape, dtype, name=name, tag=tag or name, align_bytes=64)

        lists = {}

        def load_list(name, dram):
            lists[name] = held.tile([P, N // 16], U16, name="list_" + name)
            nc.sync.dma_start(lists[name][:], dram)

        x_s = sb("x_s", [P, T], U8)
        w1_s_raw = sb("w1_s_raw", [P, H], U8)
        w2_s_raw = sb("w2_s_raw", [P, H], U8)
        x_w = sb("x_w", [P, T], U32)
        w2_raw = sb("w2_raw", [P, H], I32)
        ga_rows = sb("ga_rows", [P, P], F32)
        gb_rows = sb("gb_rows", [P, P], F32)
        identity = sb("identity", [P, P], F32)
        for plane in (x_s, w1_s_raw, w2_s_raw):
            nc.vector.memset(plane[:].bitcast(I32), 0)

        def load_gain(rows, dram):
            nc.gpsimd.memset(rows[:], 0.0)
            nc.gpsimd.dma_start(
                out=rows[0:PACK, :].rearrange("t (q r) -> t q r", r=8),
                in_=dram.rearrange("(q t r) o -> t q (r o)", t=PACK, r=8),
            )

        def turn_gain(name, rows, bank):
            turned = psum.tile([P, N], F32, name=name, tag="bank%d" % bank)
            nc.tensor.transpose(turned[:, 0:P], rows[:], identity[:])
            return turned[:, 0:PACK]

        load_gain(ga_rows, ga)
        make_identity(nc, identity[:])
        load_gain(gb_rows, gb)
        load_list("offs", offs)
        load_list("two", two)
        load_list("n1", n1)
        load_scale_rows((nc.sync, nc.scalar), x_s, x_scales)
        nc.sync.dma_start(out=x_w[:].bitcast(I32), in_=words_of(x_words))
        warm = sb("warm", [P, 1], F32)
        warm_out = sb("warm_out", [P, 1], F32)
        nc.vector.memset(warm[:], 1.0)
        nc.scalar.activation(warm_out[:], warm[:], ACT.Ln)
        w1_raw = sb("w1_raw", [P, H], I32, tag="warm")
        nc.scalar.dma_start(out=w1_raw[:], in_=words_of(w1_words))
        load_scale_rows((nc.sync,), w1_s_raw, w1_scales)
        nc.sync.dma_start(out=w2_raw[:], in_=words_of(w2_words))
        load_scale_rows((nc.sync,), w2_s_raw, w2_scales)
        for name, dram in (("n4", n4), ("n3", n3), ("n2", n2), ("n6", n6), ("n7", n7), ("n5", n5)):
            load_list(name, dram)

        xa_s = sb("xa_s", [P, S], U8)
        xb_s = sb("xb_s", [P, V], U8)
        xa_w = sb("xa_w", [P, S], U32)
        w1_d = sb("w1_d", [P, H], I32)
        w2_d = sb("w2_d", [P, H], I32)
        w1_s = sb("w1_s", [P, H], U8)
        w2_s = sb("w2_s", [P, H], U8)

        def deal(dst, src, engine=nc.gpsimd):
            engine.tensor_copy(
                out=dst[:].bitcast(I32).rearrange("p (t q i) -> p t q i", t=PACK, q=16),
                in_=src[:].bitcast(I32).rearrange("p (q t i) -> p t q i", t=PACK, q=16),
            )

        ga_ps = turn_gain("ga_ps", ga_rows, 6)
        gb_ps = turn_gain("gb_ps", gb_rows, 7)
        neg_ga, abs_ga, safe_ga, inv_ga, gb_t = [
            sb(name, [P, PACK], F32) for name in ("neg_ga", "abs_ga", "safe_ga", "inv_ga", "gb_t")
        ]
        nc.scalar.activation(neg_ga[:], ga_ps, ACT.Copy, scale=-1.0)
        nc.scalar.activation(abs_ga[:], ga_ps, ACT.Abs)
        nc.scalar.copy(gb_t[:], gb_ps)

        nc.vector.tensor_copy(xa_s[:], x_s[:].indirect(lists["offs"][:]))
        nc.vector.tensor_copy(xb_s[:], x_s[:].indirect(lists["two"][:]))
        nc.vector.tensor_copy(xa_w[:], x_w[:].indirect(lists["offs"][:]))
        deal(w1_d, w1_raw)
        deal(w1_s, w1_s_raw)

        xb_w = sb("xb_w", [P, V], U32)
        nc.vector.tensor_copy(xb_w[:], x_w[:].indirect(lists["two"][:]))
        deal(w2_d, w2_raw, nc.vector)
        deal(w2_s, w2_s_raw)

        nc.vector.tensor_scalar(safe_ga[:], abs_ga[:], TINY, None, ALU.max)
        nc.vector.reciprocal(inv_ga[:], safe_ga[:])

        def product(bank, t, st_words, st_scales, mv_words, mv_scales):
            whole = psum.tile([P, N], F32, name="acc", tag="bank%d" % bank)
            acc = whole[:, 0 : mv_words.shape[1]]
            cols = slice(t * P, (t + 1) * P)
            nc.tensor.matmul_mx(
                out=acc,
                lhsT=st_words[:, cols].bitcast(FP8X4),
                lhsT_scale=st_scales[:, cols],
                rhs=mv_words.bitcast(FP8X4),
                rhs_scale=mv_scales,
                start=True,
                stop=True,
            )
            return acc

        a_ps = [product(t, t, w1_d[:], w1_s[:], xa_w[:], xa_s[:]) for t in range(PACK)]
        b_ps = [product(PACK + t, t, w2_d[:], w2_s[:], xb_w[:], xb_s[:]) for t in range(PACK)]

        a_win = [sb("a_win%d" % t, [P, WINDOW], F32) for t in range(PACK)]
        b_win = [sb("b_win%d" % t, [P, WINDOW], F32) for t in range(PACK)]
        l_win = [sb("l_win%d" % t, [P, WINDOW], F32) for t in range(PACK)]
        a_copy = [sb("a_copy%d" % t, [P, N], F32) for t in range(PACK)]
        b_n4 = [sb("b_n4%d" % t, [P, N], F32, tag=("a_copy3", "a_win3")[t % 2]) for t in range(PACK)]
        size = [sb("size%d" % t, [P, N], F32, tag="neg_ga" if t == 0 else "") for t in range(PACK)]
        num = sb("num", [P, PACK, N], F32)
        rec = sb("rec", [P, PACK, N], F32, tag="size3")
        z2 = sb("z2", [P, PACK, N], F32)

        for t in range(PACK):
            nc.scalar.activation(a_win[t][:, 0:N], a_ps[t], ACT.Copy, scale=neg_ga[:, t : t + 1])
        for t in range(PACK):
            if t < 2:
                nc.vector.tensor_copy(a_copy[t][:], a_win[t][:, 0:N])
            else:
                nc.sync.dma_start(out=a_copy[t][:], in_=a_win[t][:, 0:N])
            nc.vector.tensor_tensor(num[:, t, :], a_win[t][:].indirect(lists["n1"][:]), a_copy[t][:], ALU.subtract)
        for t in range(PACK):
            nc.scalar.activation(size[t][:], num[:, t, :], ACT.Abs, scale=inv_ga[:, t : t + 1])
            nc.scalar.activation(l_win[t][:, 0:N], size[t][:], ACT.Ln, bias=0.5)
            nc.scalar.activation(b_win[t][:, 0:N], b_ps[t], ACT.Copy, scale=gb_t[:, t : t + 1])
        for t in range(PACK + 1):
            if t < PACK:
                nc.vector.tensor_copy(b_n4[t][:], b_win[t][:].indirect(lists["n4"][:]))
            if t > 0:
                nc.vector.tensor_tensor(
                    z2[:, t - 1, :], b_win[t - 1][:].indirect(lists["n3"][:]), b_n4[t - 1][:], ALU.subtract
                )
        for t in range(PACK):
            nc.scalar.activation(rec[:, t, :], l_win[t][:].indirect(lists["n2"][:]), ACT.Exp, scale=-1.0)

        z_bf = sb("z_bf", [P, PACK * N], BF16, tag="a_win3")
        z2_bf = sb("z2_bf", [P, PACK * N], BF16)
        nc.vector.tensor_tensor(
            z_bf[:].rearrange("p (u m k) -> p m k u", u=PACK, k=PACK),
            num[:].rearrange("p k (m u) -> p m k u", u=PACK),
            rec[:].rearrange("p k (m u) -> p m k u", u=PACK),
            ALU.mult,
        )

        def interleave(dst, src, copy=nc.scalar.copy):
            copy(
                out=dst.rearrange("p (c i k) -> p c k i", i=4, k=PACK),
                in_=src.rearrange("p k (c i) -> p c k i", i=4),
            )

        halves = (slice(0, HALF), slice(HALF, N))
        for cols in halves:
            interleave(z2_bf[:, PACK * cols.start : PACK * cols.stop], z2[:, :, cols])
        warm2 = sb("warm2", [P, 1], F32)
        nc.scalar.activation(warm2[:], z2_bf[:, PACK * N - 1 : PACK * N], ACT.Sigmoid)
        z_w = sb("z_w", [P, N], U32)
        z_s = sb("z_s", [P, N], U8)
        z2_w = sb("z2_w", [P, N], U32)
        z2_s = sb("z2_s", [P, N], U8)

        def quantize(words, scales, values, cols):
            nc.vector.quantize_mx(
                out=words[:, cols].bitcast(FP8X4),
                scales=scales[:, cols],
                in_=values[:, PACK * cols.start : PACK * cols.stop],
            )

        quantize(z2_w, z2_s, z2_bf, halves[0])
        quantize(z_w, z_s, z_bf, slice(0, P))
        quantize(z2_w, z2_s, z2_bf, halves[1])
        for t in range(1, PACK):
            quantize(z_w, z_s, z_bf, slice(t * P, (t + 1) * P))

        s_win = [sb("s_win%d" % t, [P, WINDOW], F32) for t in range(PACK)]
        s_first = [product(PACK + h, 0, z_w[:], z_s[:], z2_w[:, cols], z2_s[:, cols]) for h, cols in enumerate(halves)]
        s_ps = [None] + [product(t, t, z_w[:], z_s[:], z2_w[:], z2_s[:]) for t in range(1, PACK)]
        for h, cols in enumerate(halves):
            nc.vector.tensor_scalar(s_win[0][:, cols], s_first[h], 0.0625, None, ALU.mult)

        o_w = sb("o_w", [P, N], U32)
        o_s = sb("o_s", [P, N], U8)
        out_rows = out_0.rearrange("(p t) v -> p t v", t=PACK)
        out_words = words_of(out_1)
        res = sb("res", [P, PACK, N], F32)

        def blend(t, first, last):
            cols = slice(first, last)
            entries = slice(first // 16, last // 16)
            gate, rest, far, near = [sb("%s%d_%d" % (n, t, first), [P, last - first], F32) for n in ("gate", "rest", "far", "near")]
            nc.scalar.activation(gate[:], s_win[t][:].indirect(lists["n6"][:, entries]), ACT.Sigmoid)
            if t == 0:
                nc.vector.tensor_copy(near[:], s_win[t][:].indirect(lists["n5"][:, entries]))
                nc.vector.tensor_tensor(rest[:], s_win[t][:].indirect(lists["n7"][:, entries]), near[:], ALU.subtract)
                nc.vector.tensor_tensor(far[:], rest[:], gate[:], ALU.mult)
            else:
                nc.scalar.activation(rest[:], gate[:], ACT.Copy, scale=-1.0, bias=1.0)
                nc.vector.tensor_tensor(far[:], s_win[t][:].indirect(lists["n7"][:, entries]), gate[:], ALU.mult)
                nc.vector.tensor_tensor(near[:], s_win[t][:].indirect(lists["n5"][:, entries]), rest[:], ALU.mult)
            nc.vector.tensor_tensor(res[:, t, cols], far[:], near[:], ALU.add)
            nc.sync.dma_start(out=out_rows[:, t, cols], in_=res[:, t, cols])

        def hand_on(first, last, copy):
            cols = slice(first, last)
            o_bf = sb("o_bf%d" % first, [P, PACK * (last - first)], BF16)
            interleave(o_bf[:], res[:, :, cols], copy)
            nc.vector.quantize_mx(out=o_w[:, cols].bitcast(FP8X4), scales=o_s[:, cols], in_=o_bf[:])
            nc.sync.dma_start(out=out_words[:, cols], in_=o_w[:, cols].bitcast(I32))

        for t in range(PACK):
            if t > 0:
                nc.scalar.activation(s_win[t][:, 0:N], s_ps[t], ACT.Copy, scale=0.0625)
            if t < PACK - 1:
                blend(t, 0, N)
        blend(PACK - 1, 0, HALF)
        blend(PACK - 1, HALF, N)
        hand_on(0, HALF, nc.scalar.copy)
        hand_on(HALF, N, nc.vector.tensor_copy)
        for q in range(4):
            queue = nc.sync if q % 2 == 0 else nc.scalar
            queue.dma_start(
                out=out_2[0, 4 * q : 4 * q + 4, :].bitcast(I32),
                in_=o_s[32 * q : 32 * q + 4, :].bitcast(I32),
            )
